import numpy as np
import ml_dtypes


def mxq(x, axis, fmt="e4m3"):
    dtype, down = {"e4m3": (ml_dtypes.float8_e4m3fn, 7), "e5m2": (ml_dtypes.float8_e5m2, 14)}[fmt]
    v = np.moveaxis(np.asarray(x, np.float32).astype(ml_dtypes.bfloat16).astype(np.float64), axis, -1)
    blocks = v.reshape(v.shape[:-1] + (-1, 32))
    amax = np.abs(blocks).max(-1, keepdims=True)
    byte = np.maximum(np.where(amax > 0, np.frexp(amax)[1] - 1 + 127, 0) - down, 1)
    scale = np.exp2(byte - 127.0)
    codes = (blocks / scale).astype(np.float32).astype(dtype).astype(np.float64)
    return np.moveaxis((codes * scale).reshape(v.shape), -1, axis)


WIDE = False


def mx_kscale(k):
    if not WIDE:
        return np.ones(k)
    levels = np.array([10, -10, 5, -5, 0])
    if k % 512:
        return np.exp2(np.random.permutation(np.resize(levels, k // 32))).repeat(32)
    a = np.empty((k // 512, 16))
    for p in range(k // 512):
        a[p, :8] = np.random.permutation(np.resize(levels, 8))
        for g in range(8):
            far = levels[np.abs(levels - a[p, g]) >= 10]
            a[p, g + 8] = far[np.random.randint(len(far))]
    return np.exp2(a.ravel()).repeat(32)


def f64(x):
    return np.asarray(x).astype(np.float64)


def striped(idx):
    return np.tile(idx.reshape(-1, 16).T, (8, 1)).astype(np.uint16)


def unstriped(offs):
    return offs[:16].T.reshape(-1).astype(np.int64)


def pack_weight(w):
    k, n = w.shape
    w = f64(np.asarray(w, np.float32).astype(ml_dtypes.bfloat16)).reshape(k // 32, 32, n)
    amax = np.abs(w).max(1)
    byte = np.clip(np.where(amax > 0, np.frexp(amax)[1] - 1 + 127 - 7, 1), 1, 254)
    scaled = (w * np.exp2(127.0 - byte)[:, None, :]).reshape(k, n).astype(np.float32)
    words = np.ascontiguousarray(scaled.reshape(k // 512, 128, 4, n).transpose(0, 1, 3, 2)).astype(ml_dtypes.float8_e4m3fn).view(np.uint8)
    return words, np.ascontiguousarray(byte.astype(np.uint8).reshape(k // 512, 16, n))


def unpack_weight(words, scales):
    g, p, n, _ = words.shape
    vals = np.ascontiguousarray(words).view(ml_dtypes.float8_e4m3fn).astype(np.float64) * np.repeat(np.exp2(scales.astype(np.float64) - 127.0), 8, axis=1)[..., None]
    return vals.transpose(0, 1, 3, 2).reshape(g * 512, n)


K, T, S, N = 1024, 1024, 512, 256


def setup_inputs():
    n = np.random.standard_normal
    s = mx_kscale(K)[:, None]
    words, scales = pack_weight(n((K, N)) / np.sqrt(K) / s)
    return {
        "xT": (n((K, S)) * s).astype(np.float32),
        "w_words": words,
        "w_scales": scales,
        "gate": np.tile(np.random.uniform(0.2, 1.0, S), (N, 1)).astype(np.float32),
        "offs": striped(np.random.permutation(T)[:S]),
    }


def reference(xT, w_words, w_scales, gate, offs):
    w = unpack_weight(w_words, w_scales)
    idx = unstriped(offs)
    xq = mxq(f64(xT), 0, "e4m3")
    y = w.T @ xq
    out = np.zeros((N, T))
    out[:, idx] = f64(gate) * y
    return out

@@ -1,0 +1,120 @@
+from contextlib import ExitStack
+
+import concourse.mybir as mybir
+
+K, T, S, N = 1024, 1024, 512, 256
+FLOPS = 2 * K * S * N
+
+F32 = mybir.dt.float32
+BF16 = mybir.dt.bfloat16
+I32 = mybir.dt.int32
+U32 = mybir.dt.uint32
+U16 = mybir.dt.uint16
+U8 = mybir.dt.uint8
+FP8X4 = mybir.dt.float8_e4m3fn_x4
+MULT = mybir.AluOpType.mult
+
+P = 128
+PACK = 4
+PASSES = K // (P * PACK)
+M_TILES = N // P
+W = 128
+CHUNKS = S // W
+RUN = 4
+
+
+def tile_picked_place_lin_none_sub_l_kernel(tc, xT, w_words, w_scales, gate, offs, out):
+    nc = tc.nc
+    x_rows = xT.rearrange("(a p t) j -> a p t j", a=PASSES, t=PACK)
+    w_rows = w_words.rearrange("a p m r -> p a (m r)").bitcast(I32)
+    scale_rows = w_scales.rearrange("a (q i) m -> i q a m", i=4).bitcast(I32)
+    gate_rows = gate.rearrange("(h p) j -> p h j", p=P)
+
+    with ExitStack() as ctx:
+        keep = ctx.enter_context(tc.tile_pool(name="keep", bufs=1))
+        psum = ctx.enter_context(tc.psum_pool(name="psum", bufs=1))
+
+        offsets = keep.tile([P, S // 16], U16, name="offsets")
+        w_codes = keep.tile([P, PASSES, N], U32, name="w_codes", align_bytes=64)
+        w_planes = keep.tile([P, PASSES, N], U8, name="w_planes", align_bytes=64)
+        gates = keep.tile([P, M_TILES, S], F32, name="gates")
+        spark = keep.tile([P, 1], F32, name="spark")
+        sparked = keep.tile([P, 1], F32, name="sparked")
+        windows = [keep.tile([P, T], F32, name=f"window{h}") for h in range(M_TILES)]
+        raws = [[keep.tile([P, PACK, W], F32, name=f"raw{c}_{a}") for a in range(PASSES)] for c in range(CHUNKS)]
+        grouped = [keep.tile([P, PASSES, W * PACK], BF16, name=f"grouped{c}", align_bytes=64) for c in range(CHUNKS)]
+        codes = [keep.tile([P, PASSES, W], U32, name=f"codes{c}", align_bytes=64) for c in range(CHUNKS)]
+        planes = [keep.tile([P, PASSES, W], U8, name=f"planes{c}", align_bytes=64) for c in range(CHUNKS)]
+        banks = [[psum.tile([P, W], F32, name=f"bank{c}_{h}") for h in range(M_TILES)] for c in range(CHUNKS)]
+        sums = [[keep.tile([P, W], F32, name=f"sums{c}_{h}") for h in range(M_TILES)] for c in range(CHUNKS)]
+
+        nc.vector.memset(w_planes[:].rearrange("p a m -> p (a m)").bitcast(I32), 0)
+        nc.vector.memset(spark[:], 0.0)
+        for h in range(M_TILES):
+            nc.vector.memset(windows[h][:], 0.0)
+        nc.scalar.copy(sparked[:], spark[:])
+
+        def load_x(c):
+            for a in range(PASSES):
+                nc.sync.dma_start(raws[c][a][:], x_rows[a][:, :, c * W : (c + 1) * W])
+
+        def load_gate(j0, j1):
+            nc.sync.dma_start(gates[:, :, j0:j1], gate_rows[:, :, j0:j1])
+
+        for i in range(4):
+            nc.scalar.dma_start(w_planes[i:P:32, :, :].bitcast(I32), scale_rows[i])
+        load_x(0)
+        nc.sync.dma_start(w_codes[:].bitcast(I32), w_rows)
+        nc.sync.dma_start(offsets[:], offs)
+        load_gate(0, 2 * W)
+        load_x(1)
+        load_x(2)
+        load_gate(2 * W, S)
+        load_x(3)
+
+        def interleave(c):
+            for a in range(PASSES):
+                dst = grouped[c][:, a, :].rearrange("p (c i t) -> p c t i", i=RUN, t=PACK)
+                src = raws[c][a][:].rearrange("p t (c i) -> p c t i", i=RUN)
+                if c == 0 and a == 1:
+                    nc.vector.tensor_copy(dst, src)
+                else:
+                    nc.scalar.copy(dst, src)
+
+        def quantize(c):
+            for a in range(PASSES):
+                nc.vector.quantize_mx(out=codes[c][:, a, :].bitcast(FP8X4), scales=planes[c][:, a, :], in_=grouped[c][:, a, :])
+
+        def multiply(c):
+            for h in range(M_TILES):
+                cols = slice(h * P, (h + 1) * P)
+                for a in range(PASSES):
+                    nc.tensor.matmul_mx(
+                        out=banks[c][h][:],
+                        lhsT=w_codes[:, a, cols].bitcast(FP8X4),
+                        lhsT_scale=w_planes[:, a, cols],
+                        rhs=codes[c][:, a, :].bitcast(FP8X4),
+                        rhs_scale=planes[c][:, a, :],
+                        start=(a == 0),
+                        stop=(a == PASSES - 1),
+                    )
+                nc.scalar.copy(sums[c][h][:], banks[c][h][:])
+
+        def scatter(c, h):
+            places = offsets[:, c * (W // 16) : (c + 1) * (W // 16)]
+            nc.vector.tensor_tensor(
+                windows[h][:].indirect(places), sums[c][h][:], gates[:, h, c * W : (c + 1) * W], MULT
+            )
+
+        interleave(0)
+        quantize(0)
+        multiply(0)
+        for c in range(1, CHUNKS):
+            interleave(c)
+            scatter(c - 1, 0)
+            quantize(c)
+            multiply(c)
+            scatter(c - 1, 1)
+        for h in range(M_TILES):
+            scatter(CHUNKS - 1, h)
+            nc.sync.dma_start(out[h * P : (h + 1) * P, :], windows[h][:])

@@ -37,11 +37,20 @@ def tile_picked_place_lin_none_sub_l_kernel(tc, xT, w_words, w_scales, gate, off
         offsets = keep.tile([P, S // 16], U16, name="offsets")
         w_codes = keep.tile([P, PASSES, N], U32, name="w_codes", align_bytes=64)
         w_planes = keep.tile([P, PASSES, N], U8, name="w_planes", align_bytes=64)
-        gates = keep.tile([P, M_TILES, S], F32, name="gates")
+        gates = [keep.tile([P, M_TILES, S // 2], F32, name=f"gates{u}") for u in range(2)]
         spark = keep.tile([P, 1], F32, name="spark")
         sparked = keep.tile([P, 1], F32, name="sparked")
         windows = [keep.tile([P, T], F32, name=f"window{h}") for h in range(M_TILES)]
-        raws = [[keep.tile([P, PACK, W], F32, name=f"raw{c}_{a}") for a in range(PASSES)] for c in range(CHUNKS)]
+        loads = [(0, 1), (1, 1), (2, 2)]
+        raws = {}
+        for c0, n in loads:
+            for a in range(PASSES):
+                raws[c0, a] = keep.tile([P, PACK, n * W], F32, name=f"raw{c0}_{a}")
+        raw_of = {}
+        for c0, n in loads:
+            for a in range(PASSES):
+                for c in range(c0, c0 + n):
+                    raw_of[c, a] = raws[c0, a][:, :, (c - c0) * W : (c - c0 + 1) * W]
         grouped = [keep.tile([P, PASSES, W * PACK], BF16, name=f"grouped{c}", align_bytes=64) for c in range(CHUNKS)]
         codes = [keep.tile([P, PASSES, W], U32, name=f"codes{c}", align_bytes=64) for c in range(CHUNKS)]
         planes = [keep.tile([P, PASSES, W], U8, name=f"planes{c}", align_bytes=64) for c in range(CHUNKS)]
@@ -50,40 +59,44 @@ def tile_picked_place_lin_none_sub_l_kernel(tc, xT, w_words, w_scales, gate, off
 
         nc.vector.memset(w_planes[:].rearrange("p a m -> p (a m)").bitcast(I32), 0)
         nc.vector.memset(spark[:], 0.0)
+
+        def load_x(c0, n):
+            for a in range(PASSES):
+                nc.sync.dma_start(raws[c0, a][:], x_rows[a][:, :, c0 * W : (c0 + n) * W])
+
+        load_x(0, 1)
+        nc.sync.dma_start(w_codes[:].bitcast(I32), w_rows)
+        for i in range(4):
+            eng = nc.scalar
+            eng.dma_start(w_planes[i:P:32, :, :].bitcast(I32), scale_rows[i])
+        nc.scalar.copy(sparked[:], spark[:])
+        load_x(1, 1)
+        nc.sync.dma_start(offsets[:], offs)
+        for u in range(2):
+            nc.gpsimd.dma_start(gates[u][:], gate_rows[:, :, u * (S // 2) : (u + 1) * (S // 2)])
+        load_x(2, 2)
         for h in range(M_TILES):
             nc.vector.memset(windows[h][:], 0.0)
-        nc.scalar.copy(sparked[:], spark[:])
-
-        def load_x(c):
-            for a in range(PASSES):
-                nc.sync.dma_start(raws[c][a][:], x_rows[a][:, :, c * W : (c + 1) * W])
-
-        def load_gate(j0, j1):
-            nc.sync.dma_start(gates[:, :, j0:j1], gate_rows[:, :, j0:j1])
-
-        for i in range(4):
-            nc.scalar.dma_start(w_planes[i:P:32, :, :].bitcast(I32), scale_rows[i])
-        load_x(0)
-        nc.sync.dma_start(w_codes[:].bitcast(I32), w_rows)
-        nc.sync.dma_start(offsets[:], offs)
-        load_gate(0, 2 * W)
-        load_x(1)
-        load_x(2)
-        load_gate(2 * W, S)
-        load_x(3)
 
         def interleave(c):
             for a in range(PASSES):
                 dst = grouped[c][:, a, :].rearrange("p (c i t) -> p c t i", i=RUN, t=PACK)
-                src = raws[c][a][:].rearrange("p t (c i) -> p c t i", i=RUN)
+                src = raw_of[c, a].rearrange("p t (c i) -> p c t i", i=RUN)
                 if c == 0 and a == 1:
                     nc.vector.tensor_copy(dst, src)
                 else:
                     nc.scalar.copy(dst, src)
 
         def quantize(c):
-            for a in range(PASSES):
-                nc.vector.quantize_mx(out=codes[c][:, a, :].bitcast(FP8X4), scales=planes[c][:, a, :], in_=grouped[c][:, a, :])
+            if c == 0:
+                for a in range(PASSES):
+                    nc.vector.quantize_mx(out=codes[c][:, a, :].bitcast(FP8X4), scales=planes[c][:, a, :], in_=grouped[c][:, a, :])
+            else:
+                nc.vector.quantize_mx(
+                    out=codes[c][:].rearrange("p a w -> p (a w)").bitcast(FP8X4),
+                    scales=planes[c][:].rearrange("p a w -> p (a w)"),
+                    in_=grouped[c][:].rearrange("p a w -> p (a w)"),
+                )
 
         def multiply(c):
             for h in range(M_TILES):
@@ -102,19 +115,30 @@ def tile_picked_place_lin_none_sub_l_kernel(tc, xT, w_words, w_scales, gate, off
 
         def scatter(c, h):
             places = offsets[:, c * (W // 16) : (c + 1) * (W // 16)]
+            j0 = c % 2 * W
             nc.vector.tensor_tensor(
-                windows[h][:].indirect(places), sums[c][h][:], gates[:, h, c * W : (c + 1) * W], MULT
+                windows[h][:].indirect(places), sums[c][h][:], gates[c // 2][:, h, j0 : j0 + W], MULT
             )
 
-        interleave(0)
-        quantize(0)
-        multiply(0)
-        for c in range(1, CHUNKS):
+        def prepare(c):
             interleave(c)
-            scatter(c - 1, 0)
             quantize(c)
             multiply(c)
-            scatter(c - 1, 1)
-        for h in range(M_TILES):
-            scatter(CHUNKS - 1, h)
+
+        def store(h):
             nc.sync.dma_start(out[h * P : (h + 1) * P, :], windows[h][:])
+
+        prepare(0)
+        scatter(0, 0)
+        prepare(1)
+        scatter(0, 1)
+        scatter(1, 0)
+        prepare(2)
+        scatter(1, 1)
+        prepare(3)
+        scatter(2, 0)
+        scatter(3, 0)
+        store(0)
+        scatter(2, 1)
+        scatter(3, 1)
+        store(1)

@@ -21,6 +21,8 @@ M_TILES = N // P
 W = 128
 CHUNKS = S // W
 RUN = 4
+X_LOADS = [(0, 0, 4), (1, 0, 1), (1, 1, 2), (1, 2, 4)]
+GATE_CUTS = [(0, 128), (128, 512)]
 
 
 def tile_picked_place_lin_none_sub_l_kernel(tc, xT, w_words, w_scales, gate, offs, out):
@@ -37,20 +39,16 @@ def tile_picked_place_lin_none_sub_l_kernel(tc, xT, w_words, w_scales, gate, off
         offsets = keep.tile([P, S // 16], U16, name="offsets")
         w_codes = keep.tile([P, PASSES, N], U32, name="w_codes", align_bytes=64)
         w_planes = keep.tile([P, PASSES, N], U8, name="w_planes", align_bytes=64)
-        gates = [keep.tile([P, M_TILES, S // 2], F32, name=f"gates{u}") for u in range(2)]
+        gates = [keep.tile([P, M_TILES, hi - lo], F32, name=f"gates{lo}") for lo, hi in GATE_CUTS]
         spark = keep.tile([P, 1], F32, name="spark")
         sparked = keep.tile([P, 1], F32, name="sparked")
         windows = [keep.tile([P, T], F32, name=f"window{h}") for h in range(M_TILES)]
-        loads = [(0, 1), (1, 1), (2, 2)]
-        raws = {}
-        for c0, n in loads:
-            for a in range(PASSES):
-                raws[c0, a] = keep.tile([P, PACK, n * W], F32, name=f"raw{c0}_{a}")
+        raws = []
         raw_of = {}
-        for c0, n in loads:
-            for a in range(PASSES):
-                for c in range(c0, c0 + n):
-                    raw_of[c, a] = raws[c0, a][:, :, (c - c0) * W : (c - c0 + 1) * W]
+        for n, (a, lo, hi) in enumerate(X_LOADS):
+            raws.append(keep.tile([P, PACK, (hi - lo) * W], F32, name=f"raw{n}"))
+            for c in range(lo, hi):
+                raw_of[c, a] = raws[n][:, :, (c - lo) * W : (c - lo + 1) * W]
         grouped = [keep.tile([P, PASSES, W * PACK], BF16, name=f"grouped{c}", align_bytes=64) for c in range(CHUNKS)]
         codes = [keep.tile([P, PASSES, W], U32, name=f"codes{c}", align_bytes=64) for c in range(CHUNKS)]
         planes = [keep.tile([P, PASSES, W], U8, name=f"planes{c}", align_bytes=64) for c in range(CHUNKS)]
@@ -59,44 +57,39 @@ def tile_picked_place_lin_none_sub_l_kernel(tc, xT, w_words, w_scales, gate, off
 
         nc.vector.memset(w_planes[:].rearrange("p a m -> p (a m)").bitcast(I32), 0)
         nc.vector.memset(spark[:], 0.0)
-
-        def load_x(c0, n):
-            for a in range(PASSES):
-                nc.sync.dma_start(raws[c0, a][:], x_rows[a][:, :, c0 * W : (c0 + n) * W])
-
-        load_x(0, 1)
-        nc.sync.dma_start(w_codes[:].bitcast(I32), w_rows)
-        for i in range(4):
-            eng = nc.scalar
-            eng.dma_start(w_planes[i:P:32, :, :].bitcast(I32), scale_rows[i])
         nc.scalar.copy(sparked[:], spark[:])
-        load_x(1, 1)
+
+        def load_x(n):
+            a, lo, hi = X_LOADS[n]
+            nc.sync.dma_start(raws[n][:], x_rows[a][:, :, lo * W : hi * W])
+
+        def load_gate(u, queue):
+            lo, hi = GATE_CUTS[u]
+            queue.dma_start(gates[u][:], gate_rows[:, :, lo:hi])
+
+        load_x(0)
+        load_x(1)
         nc.sync.dma_start(offsets[:], offs)
-        for u in range(2):
-            nc.gpsimd.dma_start(gates[u][:], gate_rows[:, :, u * (S // 2) : (u + 1) * (S // 2)])
-        load_x(2, 2)
+        for i in range(4):
+            nc.sync.dma_start(w_planes[i:P:32, :, :].bitcast(I32), scale_rows[i])
+        nc.sync.dma_start(w_codes[:].bitcast(I32), w_rows)
+        load_gate(0, nc.gpsimd)
+        load_x(2)
+        load_x(3)
+        load_gate(1, nc.sync)
         for h in range(M_TILES):
             nc.vector.memset(windows[h][:], 0.0)
 
-        def interleave(c):
-            for a in range(PASSES):
-                dst = grouped[c][:, a, :].rearrange("p (c i t) -> p c t i", i=RUN, t=PACK)
-                src = raw_of[c, a].rearrange("p t (c i) -> p c t i", i=RUN)
-                if c == 0 and a == 1:
-                    nc.vector.tensor_copy(dst, src)
-                else:
-                    nc.scalar.copy(dst, src)
-
-        def quantize(c):
-            if c == 0:
-                for a in range(PASSES):
-                    nc.vector.quantize_mx(out=codes[c][:, a, :].bitcast(FP8X4), scales=planes[c][:, a, :], in_=grouped[c][:, a, :])
+        def pack(c, a):
+            dst = grouped[c][:, a, :].rearrange("p (c i t) -> p c t i", i=RUN, t=PACK)
+            src = raw_of[c, a].rearrange("p t (c i) -> p c t i", i=RUN)
+            if (c, a) in [(0, 0), (2, 0), (0, 1)]:
+                nc.vector.tensor_copy(dst, src)
             else:
-                nc.vector.quantize_mx(
-                    out=codes[c][:].rearrange("p a w -> p (a w)").bitcast(FP8X4),
-                    scales=planes[c][:].rearrange("p a w -> p (a w)"),
-                    in_=grouped[c][:].rearrange("p a w -> p (a w)"),
-                )
+                nc.scalar.copy(dst, src)
+
+        def quantize(c, a):
+            nc.vector.quantize_mx(out=codes[c][:, a, :].bitcast(FP8X4), scales=planes[c][:, a, :], in_=grouped[c][:, a, :])
 
         def multiply(c):
             for h in range(M_TILES):
@@ -115,27 +108,39 @@ def tile_picked_place_lin_none_sub_l_kernel(tc, xT, w_words, w_scales, gate, off
 
         def scatter(c, h):
             places = offsets[:, c * (W // 16) : (c + 1) * (W // 16)]
-            j0 = c % 2 * W
+            u = 0 if c == 0 else 1
+            j0 = c * W - GATE_CUTS[u][0]
             nc.vector.tensor_tensor(
-                windows[h][:].indirect(places), sums[c][h][:], gates[c // 2][:, h, j0 : j0 + W], MULT
+                windows[h][:].indirect(places), sums[c][h][:], gates[u][:, h, j0 : j0 + W], MULT
             )
-
-        def prepare(c):
-            interleave(c)
-            quantize(c)
-            multiply(c)
 
         def store(h):
             nc.sync.dma_start(out[h * P : (h + 1) * P, :], windows[h][:])
 
-        prepare(0)
+        pack(0, 0)
+        pack(1, 0)
+        quantize(0, 0)
+        pack(2, 0)
+        quantize(1, 0)
+        pack(3, 0)
+        pack(0, 1)
+        quantize(0, 1)
+        multiply(0)
+        quantize(2, 0)
+        quantize(3, 0)
         scatter(0, 0)
-        prepare(1)
+        pack(1, 1)
+        quantize(1, 1)
+        multiply(1)
         scatter(0, 1)
         scatter(1, 0)
-        prepare(2)
+        pack(2, 1)
+        quantize(2, 1)
+        multiply(2)
         scatter(1, 1)
-        prepare(3)
+        pack(3, 1)
+        quantize(3, 1)
+        multiply(3)
         scatter(2, 0)
         scatter(3, 0)
         store(0)

@@ -21,8 +21,8 @@ M_TILES = N // P
 W = 128
 CHUNKS = S // W
 RUN = 4
-X_LOADS = [(0, 0, 4), (1, 0, 1), (1, 1, 2), (1, 2, 4)]
-GATE_CUTS = [(0, 128), (128, 512)]
+X_LOADS = [(0, 0, 2), (1, 0, 1), (1, 1, 2), (0, 2, 4), (1, 2, 3), (1, 3, 4)]
+GATE_CUTS = [(0, 256), (256, 512)]
 
 
 def tile_picked_place_lin_none_sub_l_kernel(tc, xT, w_words, w_scales, gate, offs, out):
@@ -69,27 +69,35 @@ def tile_picked_place_lin_none_sub_l_kernel(tc, xT, w_words, w_scales, gate, off
 
         load_x(0)
         load_x(1)
-        nc.sync.dma_start(offsets[:], offs)
+        nc.sync.dma_start(w_codes[:].bitcast(I32), w_rows)
         for i in range(4):
             nc.sync.dma_start(w_planes[i:P:32, :, :].bitcast(I32), scale_rows[i])
-        nc.sync.dma_start(w_codes[:].bitcast(I32), w_rows)
-        load_gate(0, nc.gpsimd)
         load_x(2)
-        load_x(3)
-        load_gate(1, nc.sync)
+        nc.sync.dma_start(offsets[:], offs)
+        for u in range(2):
+            load_gate(u, nc.gpsimd)
+        for n in range(3, len(X_LOADS)):
+            load_x(n)
         for h in range(M_TILES):
             nc.vector.memset(windows[h][:], 0.0)
 
         def pack(c, a):
             dst = grouped[c][:, a, :].rearrange("p (c i t) -> p c t i", i=RUN, t=PACK)
             src = raw_of[c, a].rearrange("p t (c i) -> p c t i", i=RUN)
-            if (c, a) in [(0, 0), (2, 0), (0, 1)]:
+            if (c, a) in [(0, 0), (0, 1), (1, 1)]:
                 nc.vector.tensor_copy(dst, src)
             else:
                 nc.scalar.copy(dst, src)
 
         def quantize(c, a):
             nc.vector.quantize_mx(out=codes[c][:, a, :].bitcast(FP8X4), scales=planes[c][:, a, :], in_=grouped[c][:, a, :])
+
+        def quantize_both(c):
+            nc.vector.quantize_mx(
+                out=codes[c][:].rearrange("p a w -> p (a w)").bitcast(FP8X4),
+                scales=planes[c][:].rearrange("p a w -> p (a w)"),
+                in_=grouped[c][:].rearrange("p a w -> p (a w)"),
+            )
 
         def multiply(c):
             for h in range(M_TILES):
@@ -108,7 +116,7 @@ def tile_picked_place_lin_none_sub_l_kernel(tc, xT, w_words, w_scales, gate, off
 
         def scatter(c, h):
             places = offsets[:, c * (W // 16) : (c + 1) * (W // 16)]
-            u = 0 if c == 0 else 1
+            u = c // 2
             j0 = c * W - GATE_CUTS[u][0]
             nc.vector.tensor_tensor(
                 windows[h][:].indirect(places), sums[c][h][:], gates[u][:, h, j0 : j0 + W], MULT
@@ -118,28 +126,26 @@ def tile_picked_place_lin_none_sub_l_kernel(tc, xT, w_words, w_scales, gate, off
             nc.sync.dma_start(out[h * P : (h + 1) * P, :], windows[h][:])
 
         pack(0, 0)
-        pack(1, 0)
         quantize(0, 0)
-        pack(2, 0)
-        quantize(1, 0)
-        pack(3, 0)
+        pack(1, 0)
         pack(0, 1)
         quantize(0, 1)
         multiply(0)
-        quantize(2, 0)
-        quantize(3, 0)
-        scatter(0, 0)
+        quantize(1, 0)
         pack(1, 1)
         quantize(1, 1)
+        scatter(0, 0)
         multiply(1)
         scatter(0, 1)
         scatter(1, 0)
-        pack(2, 1)
-        quantize(2, 1)
+        for a in range(PASSES):
+            pack(2, a)
+        quantize_both(2)
         multiply(2)
         scatter(1, 1)
-        pack(3, 1)
-        quantize(3, 1)
+        for a in range(PASSES):
+            pack(3, a)
+        quantize_both(3)
         multiply(3)
         scatter(2, 0)
         scatter(3, 0)

from contextlib import ExitStack

import concourse.mybir as mybir

K, T, S, N = 1024, 1024, 512, 256
FLOPS = 2 * K * S * N

F32 = mybir.dt.float32
BF16 = mybir.dt.bfloat16
I32 = mybir.dt.int32
U32 = mybir.dt.uint32
U16 = mybir.dt.uint16
U8 = mybir.dt.uint8
FP8X4 = mybir.dt.float8_e4m3fn_x4
MULT = mybir.AluOpType.mult

P = 128
PACK = 4
PASSES = K // (P * PACK)
M_TILES = N // P
W = 128
CHUNKS = S // W
RUN = 4
X_LOADS = [(0, 0, 2), (1, 0, 1), (1, 1, 2), (0, 2, 4), (1, 2, 3), (1, 3, 4)]
GATE_CUTS = [(0, 256), (256, 512)]


def tile_picked_place_lin_none_sub_l_kernel(tc, xT, w_words, w_scales, gate, offs, out):
    nc = tc.nc
    x_rows = xT.rearrange("(a p t) j -> a p t j", a=PASSES, t=PACK)
    w_rows = w_words.rearrange("a p m r -> p a (m r)").bitcast(I32)
    scale_rows = w_scales.rearrange("a (q i) m -> i q a m", i=4).bitcast(I32)
    gate_rows = gate.rearrange("(h p) j -> p h j", p=P)

    with ExitStack() as ctx:
        keep = ctx.enter_context(tc.tile_pool(name="keep", bufs=1))
        psum = ctx.enter_context(tc.psum_pool(name="psum", bufs=1))

        offsets = keep.tile([P, S // 16], U16, name="offsets")
        w_codes = keep.tile([P, PASSES, N], U32, name="w_codes", align_bytes=64)
        w_planes = keep.tile([P, PASSES, N], U8, name="w_planes", align_bytes=64)
        gates = [keep.tile([P, M_TILES, hi - lo], F32, name=f"gates{lo}") for lo, hi in GATE_CUTS]
        spark = keep.tile([P, 1], F32, name="spark")
        sparked = keep.tile([P, 1], F32, name="sparked")
        windows = [keep.tile([P, T], F32, name=f"window{h}") for h in range(M_TILES)]
        raws = []
        raw_of = {}
        for n, (a, lo, hi) in enumerate(X_LOADS):
            raws.append(keep.tile([P, PACK, (hi - lo) * W], F32, name=f"raw{n}"))
            for c in range(lo, hi):
                raw_of[c, a] = raws[n][:, :, (c - lo) * W : (c - lo + 1) * W]
        grouped = [keep.tile([P, PASSES, W * PACK], BF16, name=f"grouped{c}", align_bytes=64) for c in range(CHUNKS)]
        codes = [keep.tile([P, PASSES, W], U32, name=f"codes{c}", align_bytes=64) for c in range(CHUNKS)]
        planes = [keep.tile([P, PASSES, W], U8, name=f"planes{c}", align_bytes=64) for c in range(CHUNKS)]
        banks = [[psum.tile([P, W], F32, name=f"bank{c}_{h}") for h in range(M_TILES)] for c in range(CHUNKS)]
        sums = [[keep.tile([P, W], F32, name=f"sums{c}_{h}") for h in range(M_TILES)] for c in range(CHUNKS)]

        nc.vector.memset(w_planes[:].rearrange("p a m -> p (a m)").bitcast(I32), 0)
        nc.vector.memset(spark[:], 0.0)
        nc.scalar.copy(sparked[:], spark[:])

        def load_x(n):
            a, lo, hi = X_LOADS[n]
            nc.sync.dma_start(raws[n][:], x_rows[a][:, :, lo * W : hi * W])

        def load_gate(u, queue):
            lo, hi = GATE_CUTS[u]
            queue.dma_start(gates[u][:], gate_rows[:, :, lo:hi])

        load_x(0)
        load_x(1)
        nc.sync.dma_start(w_codes[:].bitcast(I32), w_rows)
        for i in range(4):
            nc.sync.dma_start(w_planes[i:P:32, :, :].bitcast(I32), scale_rows[i])
        load_x(2)
        nc.sync.dma_start(offsets[:], offs)
        for u in range(2):
            load_gate(u, nc.gpsimd)
        for n in range(3, len(X_LOADS)):
            load_x(n)
        for h in range(M_TILES):
            nc.vector.memset(windows[h][:], 0.0)

        def pack(c, a):
            dst = grouped[c][:, a, :].rearrange("p (c i t) -> p c t i", i=RUN, t=PACK)
            src = raw_of[c, a].rearrange("p t (c i) -> p c t i", i=RUN)
            if (c, a) in [(0, 0), (0, 1), (1, 1)]:
                nc.vector.tensor_copy(dst, src)
            else:
                nc.scalar.copy(dst, src)

        def quantize(c, a):
            nc.vector.quantize_mx(out=codes[c][:, a, :].bitcast(FP8X4), scales=planes[c][:, a, :], in_=grouped[c][:, a, :])

        def quantize_both(c):
            nc.vector.quantize_mx(
                out=codes[c][:].rearrange("p a w -> p (a w)").bitcast(FP8X4),
                scales=planes[c][:].rearrange("p a w -> p (a w)"),
                in_=grouped[c][:].rearrange("p a w -> p (a w)"),
            )

        def multiply(c):
            for h in range(M_TILES):
                cols = slice(h * P, (h + 1) * P)
                for a in range(PASSES):
                    nc.tensor.matmul_mx(
                        out=banks[c][h][:],
                        lhsT=w_codes[:, a, cols].bitcast(FP8X4),
                        lhsT_scale=w_planes[:, a, cols],
                        rhs=codes[c][:, a, :].bitcast(FP8X4),
                        rhs_scale=planes[c][:, a, :],
                        start=(a == 0),
                        stop=(a == PASSES - 1),
                    )
                nc.scalar.copy(sums[c][h][:], banks[c][h][:])

        def scatter(c, h):
            places = offsets[:, c * (W // 16) : (c + 1) * (W // 16)]
            u = c // 2
            j0 = c * W - GATE_CUTS[u][0]
            nc.vector.tensor_tensor(
                windows[h][:].indirect(places), sums[c][h][:], gates[u][:, h, j0 : j0 + W], MULT
            )

        def store(h):
            nc.sync.dma_start(out[h * P : (h + 1) * P, :], windows[h][:])

        pack(0, 0)
        quantize(0, 0)
        pack(1, 0)
        pack(0, 1)
        quantize(0, 1)
        multiply(0)
        quantize(1, 0)
        pack(1, 1)
        quantize(1, 1)
        scatter(0, 0)
        multiply(1)
        scatter(0, 1)
        scatter(1, 0)
        for a in range(PASSES):
            pack(2, a)
        quantize_both(2)
        multiply(2)
        scatter(1, 1)
        for a in range(PASSES):
            pack(3, a)
        quantize_both(3)
        multiply(3)
        scatter(2, 0)
        scatter(3, 0)
        store(0)
        scatter(2, 1)
        scatter(3, 1)
        store(1)
